import numpy as np
import ml_dtypes


def mxq(x, axis, fmt="e4m3"):
    dtype, down = {"e4m3": (ml_dtypes.float8_e4m3fn, 7), "e5m2": (ml_dtypes.float8_e5m2, 14)}[fmt]
    v = np.moveaxis(np.asarray(x, np.float32).astype(ml_dtypes.bfloat16).astype(np.float64), axis, -1)
    blocks = v.reshape(v.shape[:-1] + (-1, 32))
    amax = np.abs(blocks).max(-1, keepdims=True)
    byte = np.maximum(np.where(amax > 0, np.frexp(amax)[1] - 1 + 127, 0) - down, 1)
    scale = np.exp2(byte - 127.0)
    codes = (blocks / scale).astype(np.float32).astype(dtype).astype(np.float64)
    return np.moveaxis((codes * scale).reshape(v.shape), -1, axis)


WIDE = False


def mx_kscale(k):
    if not WIDE:
        return np.ones(k)
    levels = np.array([30, -30])
    if k % 512:
        return np.exp2(np.random.permutation(np.resize(levels, k // 32))).repeat(32)
    a = np.empty((k // 512, 16))
    for p in range(k // 512):
        a[p, :8] = np.random.permutation(np.resize(levels, 8))
        for g in range(8):
            far = levels[np.abs(levels - a[p, g]) >= 10]
            a[p, g + 8] = far[np.random.randint(len(far))]
    return np.exp2(a.ravel()).repeat(32)


def f64(x):
    return np.asarray(x).astype(np.float64)


def striped(idx):
    return np.tile(np.asarray(idx).reshape(-1, 16).T, (8, 1)).astype(np.uint16)


def unstriped(offs):
    return offs[:16].T.reshape(-1).astype(np.int64)


E2M1 = np.array([0.0, 0.5, 1.0, 1.5, 2.0, 3.0, 4.0, 6.0, -0.0, -0.5, -1.0, -1.5, -2.0, -3.0, -4.0, -6.0])


def pack_weight(w, fmt):
    k, n = w.shape
    w = f64(np.asarray(w, np.float32).astype(ml_dtypes.bfloat16)).reshape(k // 32, 32, n)
    amax = np.abs(w).max(1)
    if fmt in ("e4m3", "e5m2"):
        byte = np.frexp(amax)[1] - 1 + 127 - (7 if fmt == "e4m3" else 14)
    else:
        mant, ex = np.frexp(amax / 6.0)
        byte = np.where(mant > 0.5, ex, ex - 1) + 127
    byte = np.clip(np.where(amax > 0, byte, 1), 1, 254)
    scaled = (w * np.exp2(127.0 - byte)[:, None, :]).reshape(k, n).astype(np.float32)
    by_word = np.ascontiguousarray(scaled.reshape(k // 512, 128, 4, n).transpose(0, 1, 3, 2))
    if fmt in ("e4m3", "e5m2"):
        words = by_word.astype(ml_dtypes.float8_e4m3fn if fmt == "e4m3" else ml_dtypes.float8_e5m2).view(np.uint8)
    else:
        c = by_word.astype(ml_dtypes.float4_e2m1fn).view(np.uint8) & 0xF
        words = (c[..., 0::2] | (c[..., 1::2] << 4)).reshape(k // 512, 128, 2 * n)
    return np.ascontiguousarray(words), np.ascontiguousarray(byte.astype(np.uint8).reshape(k // 512, 16, n))


def unpack_weight(words, scales, fmt):
    g, _, n = scales.shape
    words = np.ascontiguousarray(words).reshape(g, 128, n, -1)
    if fmt in ("e4m3", "e5m2"):
        vals = words.view(ml_dtypes.float8_e4m3fn if fmt == "e4m3" else ml_dtypes.float8_e5m2).astype(np.float64)
    else:
        nib = np.empty((g, 128, n, 4), np.uint8)
        nib[..., 0::2] = words & 0xF
        nib[..., 1::2] = words >> 4
        vals = E2M1[nib]
    vals = vals * np.repeat(np.exp2(scales.astype(np.float64) - 127.0), 8, axis=1)[..., None]
    return vals.transpose(0, 1, 3, 2).reshape(g * 512, n)


def bf(x):
    return np.asarray(x, np.float32).astype(ml_dtypes.bfloat16)


def planes(Y):
    r, m = Y.shape
    b = f64(bf(Y)).reshape(r // 32, 32, m)
    amax = np.abs(b).max(1)
    byte = np.clip(np.where(amax > 0, np.frexp(amax)[1] - 1 + 127 - 7, 1), 1, 254)
    codes = (b * np.exp2(127.0 - byte)[:, None, :]).reshape(r, m).astype(np.float32).astype(ml_dtypes.float8_e4m3fn).view(np.uint8)
    words = codes.reshape(r // 512, 128, 4, m).transpose(0, 1, 3, 2)
    return np.ascontiguousarray(words), np.ascontiguousarray(byte.astype(np.uint8).reshape(r // 512, 16, m))


K, T, J, R, V, N = 1024, 512, 128, 512, 512, 512


def setup_inputs():
    n = np.random.standard_normal
    idx = np.random.permutation(T)[:J]
    idx2 = np.random.permutation(V)[:J]
    idx3 = np.random.permutation(V)[:J]
    fk = mx_kscale(K)
    fr = mx_kscale(R)
    xtp = pack_weight(n((K, T)) / fk[:, None], "e2m1")
    wp = pack_weight(n((K, R)) * 1 / np.sqrt(K) * fk[:, None] * fr, "e5m2")
    return {
        "xt_words": xtp[0],
        "xt_scales": xtp[1],
        "w_words": wp[0],
        "w_scales": wp[1],
        "tb": (n((R, V)) * 0.7 * fr[:, None]).astype(np.float32),
        "wb": (n((R, N)) * 1 / np.sqrt(R) / fr[:, None]).astype(np.float32),
        "rs": (n((N, J))).astype(np.float32),
        "gm": (np.random.uniform(0.5, 2.0, (N, 1))).astype(np.float32),
        "offs": striped(idx),
        "offs2": striped(idx2),
        "offs3": striped(idx3),
    }


def reference(xt_words, xt_scales, w_words, w_scales, tb, wb, rs, gm, offs, offs2, offs3):
    idx = unstriped(offs)
    idx2 = unstriped(offs2)
    idx3 = unstriped(offs3)
    xtu = unpack_weight(xt_words, xt_scales, "e2m1")
    wu = unpack_weight(w_words, w_scales, "e5m2")
    xtidxg = xtu[:, idx]
    a = wu.T @ xtidxg
    hid = np.maximum(a + f64(tb)[:, idx2] - f64(tb)[:, idx3], 0.0)
    wbq = mxq(f64(wb), 0, "e4m3")
    hidq = mxq(hid, 0, "e5m2")
    p = wbq.T @ hidq
    y = f64(gm) * p + f64(rs)
    words, scales = planes(y)
    return y, words, scales

@@ -1,0 +1,159 @@
+from contextlib import ExitStack
+
+import concourse.mybir as mybir
+from concourse.masks import make_identity
+
+K, T, J, R, V, N = 1024, 512, 128, 512, 512, 512
+FLOPS = 2 * K * R * J + 2 * R * N * J
+
+F32 = mybir.dt.float32
+BF16 = mybir.dt.bfloat16
+I32 = mybir.dt.int32
+U32 = mybir.dt.uint32
+U16 = mybir.dt.uint16
+U8 = mybir.dt.uint8
+E4M3 = mybir.dt.float8_e4m3fn_x4
+E5M2 = mybir.dt.float8_e5m2_x4
+E2M1 = mybir.dt.float4_e2m1fn_x4
+ALU = mybir.AluOpType
+COPY = mybir.ActivationFunctionType.Copy
+
+P = 128
+PACK = 4
+PASSES = K // (P * PACK)
+HALVES = 2
+HALF = N // HALVES
+HM = HALF // PACK
+
+
+def tile_list_picked_tworeach_residual_pl_kernel(
+    tc, xt_words, xt_scales, w_words, w_scales, tb, wb, rs, gm, offs, offs2, offs3, out_0, out_1, out_2
+):
+    nc = tc.nc
+    with ExitStack() as ctx:
+        sb = ctx.enter_context(tc.tile_pool(name="sb", bufs=1))
+        ps = ctx.enter_context(tc.psum_pool(name="ps", bufs=1))
+
+        idx = sb.tile([P, J // 16], U16, name="idx")
+        idx2 = sb.tile([P, J // 16], U16, name="idx2")
+        idx3 = sb.tile([P, J // 16], U16, name="idx3")
+        xw = [sb.tile([P, T], U16, name="xw%d" % z, align_bytes=64) for z in range(PASSES)]
+        xs = sb.tile([P, PASSES, T], U8, name="xs", align_bytes=64)
+        ww = sb.tile([P, PASSES, R], U32, name="ww", align_bytes=64)
+        ws = sb.tile([P, PASSES, R], U8, name="ws", align_bytes=64)
+        tbt = [sb.tile([P, V], F32, name="tb%d" % t, align_bytes=64) for t in range(PACK)]
+        wraw = [sb.tile([P, PACK, HALF], F32, name="wraw%d" % h, align_bytes=64) for h in range(HALVES)]
+        rst = sb.tile([P, PACK, J], F32, name="rst", align_bytes=64)
+        gmt = sb.tile([P, PACK], F32, name="gmt", align_bytes=64)
+        ident = sb.tile([P, P], F32, name="ident", align_bytes=64)
+
+        nc.vector.memset(xs[:].rearrange("p z c -> p (z c)").bitcast(I32), 0)
+        nc.vector.memset(ws[:].rearrange("p z c -> p (z c)").bitcast(I32), 0)
+
+        nc.sync.dma_start(idx[:], offs)
+        for z in range(PASSES):
+            nc.sync.dma_start(xw[z][:].bitcast(I32), xt_words[z].bitcast(I32))
+        for q in range(4):
+            nc.scalar.dma_start(
+                xs[32 * q : 32 * q + 4, :, :].bitcast(I32),
+                xt_scales[:, 4 * q : 4 * q + 4, :].rearrange("z r c -> r z c").bitcast(I32),
+            )
+        nc.sync.dma_start(ww[:].bitcast(I32), w_words.rearrange("z p c r -> p z (c r)").bitcast(I32))
+        for q in range(4):
+            queue = nc.gpsimd if q < 2 else nc.scalar
+            queue.dma_start(
+                ws[32 * q : 32 * q + 4, :, :].bitcast(I32),
+                w_scales[:, 4 * q : 4 * q + 4, :].rearrange("z r c -> r z c").bitcast(I32),
+            )
+        tb_rows = tb.rearrange("(p t) v -> p t v", t=PACK)
+        nc.sync.dma_start(tbt[0][:], tb_rows[:, 0, :])
+        nc.sync.dma_start(idx3[:], offs3)
+        nc.sync.dma_start(idx2[:], offs2)
+        for t in range(1, PACK):
+            nc.sync.dma_start(tbt[t][:], tb_rows[:, t, :])
+        wb_rows = wb.rearrange("(p i) n -> p i n", i=PACK)
+        for h in range(HALVES):
+            nc.sync.dma_start(wraw[h][:], wb_rows[:, :, h * HALF : (h + 1) * HALF])
+        nc.sync.dma_start(rst[:], rs.rearrange("(p t) j -> p t j", t=PACK))
+        nc.sync.dma_start(gmt[:], gm.rearrange("(p t) o -> p (t o)", t=PACK))
+        make_identity(nc, ident[:])
+
+        xg = sb.tile([P, PASSES, J], U16, name="xg", align_bytes=64)
+        xsg = sb.tile([P, PASSES, J], U8, name="xsg", align_bytes=64)
+        for z in range(PASSES):
+            nc.vector.tensor_copy(xg[:, z, :], xw[z][:].indirect(idx[:]))
+        for z in range(PASSES):
+            nc.vector.tensor_copy(xsg[:, z, :], xs[:, z, :].indirect(idx[:]))
+        a_jr = ps.tile([P, R], F32, name="a_jr")
+        for z in range(PASSES):
+            nc.tensor.matmul_mx(
+                out=a_jr[:],
+                lhsT=xg[:, z, :].bitcast(E2M1),
+                lhsT_scale=xsg[:, z, :],
+                rhs=ww[:, z, :].bitcast(E5M2),
+                rhs_scale=ws[:, z, :],
+                start=(z == 0),
+                stop=(z == PASSES - 1),
+            )
+        g3 = sb.tile([P, PACK, J], F32, name="g3", align_bytes=64)
+        d = sb.tile([P, PACK, J], F32, name="d", align_bytes=64)
+        a_dealt = sb.tile([P, PACK, P], F32, name="a_dealt", align_bytes=64)
+        for t in range(PACK):
+            nc.scalar.activation(g3[:, t, :], tbt[t][:].indirect(idx3[:]), COPY)
+            nc.vector.tensor_tensor(d[:, t, :], tbt[t][:].indirect(idx2[:]), g3[:, t, :], ALU.subtract)
+        nc.scalar.copy(a_dealt[:], a_jr[:].rearrange("j (m t) -> j t m", t=PACK))
+        a_rj = ps.tile([P, PACK, J], F32, name="a_rj")
+        for t in range(PACK):
+            nc.tensor.transpose(a_rj[:, t, :], a_dealt[:, t, :], ident[:])
+        pre = sb.tile([P, PACK, J], F32, name="pre", align_bytes=64)
+        nc.vector.tensor_tensor(pre[:], a_rj[:], d[:], ALU.add)
+        hid = sb.tile([P, J, PACK], BF16, name="hid", align_bytes=64)
+        nc.vector.tensor_scalar_max(
+            hid[:].rearrange("p (c i) t -> p c t i", i=4), pre[:].rearrange("p t (c i) -> p c t i", i=4), 0.0
+        )
+        hq = sb.tile([P, J], U32, name="hq", align_bytes=64)
+        hs = sb.tile([P, J], U8, name="hs", align_bytes=64)
+        nc.vector.quantize_mx(out=hq[:].bitcast(E5M2), scales=hs[:], in_=hid[:].rearrange("p j t -> p (j t)"))
+
+        wq = sb.tile([P, PACK, P], U32, name="wq", align_bytes=64)
+        wqs = sb.tile([P, PACK, P], U8, name="wqs", align_bytes=64)
+        for h in range(HALVES):
+            wbf = sb.tile([P, PACK, HM, PACK], BF16, name="wbf%d" % h, align_bytes=64)
+            dst = wbf[:].rearrange("p t m i -> p m t i")
+            src = wraw[h][:].rearrange("p i (m t) -> p m t i", t=PACK)
+            if h == 0:
+                nc.scalar.copy(dst, src)
+            else:
+                nc.vector.tensor_copy(dst, src)
+            for t in range(PACK):
+                nc.vector.quantize_mx(
+                    out=wq[:, t, h * HM : (h + 1) * HM].bitcast(E4M3),
+                    scales=wqs[:, t, h * HM : (h + 1) * HM],
+                    in_=wbf[:, t, :, :].rearrange("p m i -> p (m i)"),
+                )
+
+        y = sb.tile([P, PACK, J], F32, name="y", align_bytes=64)
+        for t in range(PACK):
+            pt = ps.tile([P, J], F32, name="pt%d" % t)
+            nc.tensor.matmul_mx(
+                out=pt[:],
+                lhsT=wq[:, t, :].bitcast(E4M3),
+                lhsT_scale=wqs[:, t, :],
+                rhs=hq[:].bitcast(E5M2),
+                rhs_scale=hs[:],
+                start=True,
+                stop=True,
+            )
+            nc.vector.scalar_tensor_tensor(y[:, t, :], pt[:], gmt[:, t : t + 1], rst[:, t, :], ALU.mult, ALU.add)
+        nc.sync.dma_start(out_0.rearrange("(p t) j -> p t j", t=PACK), y[:])
+        yb = sb.tile([P, J, PACK], BF16, name="yb", align_bytes=64)
+        nc.vector.tensor_copy(
+            yb[:].rearrange("p (c i) t -> p c t i", i=4), y[:].rearrange("p t (c i) -> p c t i", i=4)
+        )
+        yq = sb.tile([P, J], U32, name="yq", align_bytes=64)
+        ys = sb.tile([P, J], U8, name="ys", align_bytes=64)
+        nc.vector.quantize_mx(out=yq[:].bitcast(E4M3), scales=ys[:], in_=yb[:].rearrange("p j t -> p (j t)"))
+        nc.sync.dma_start(out_1[0].rearrange("p c r -> p (c r)").bitcast(I32), yq[:].bitcast(I32))
+        for q in range(4):
+            queue = nc.scalar if q % 2 == 0 else nc.sync
+            queue.dma_start(out_2[0, 4 * q : 4 * q + 4, :].bitcast(I32), ys[32 * q : 32 * q + 4, :].bitcast(I32))

@@ -17,6 +17,7 @@ E5M2 = mybir.dt.float8_e5m2_x4
 E2M1 = mybir.dt.float4_e2m1fn_x4
 ALU = mybir.AluOpType
 COPY = mybir.ActivationFunctionType.Copy
+RELU = mybir.ActivationFunctionType.Relu
 
 P = 128
 PACK = 4
@@ -37,51 +38,53 @@ def tile_list_picked_tworeach_residual_pl_kernel(
         idx = sb.tile([P, J // 16], U16, name="idx")
         idx2 = sb.tile([P, J // 16], U16, name="idx2")
         idx3 = sb.tile([P, J // 16], U16, name="idx3")
-        xw = [sb.tile([P, T], U16, name="xw%d" % z, align_bytes=64) for z in range(PASSES)]
+        xw = sb.tile([P, PASSES * T], U16, name="xw", align_bytes=64)
+        xw1 = sb.tile([P, T], U16, name="xw1", align_bytes=64)
         xs = sb.tile([P, PASSES, T], U8, name="xs", align_bytes=64)
         ww = sb.tile([P, PASSES, R], U32, name="ww", align_bytes=64)
         ws = sb.tile([P, PASSES, R], U8, name="ws", align_bytes=64)
-        tbt = [sb.tile([P, V], F32, name="tb%d" % t, align_bytes=64) for t in range(PACK)]
+        tb01 = sb.tile([P, 2, V], F32, name="tb01", align_bytes=64)
+        tb23 = sb.tile([P, 2, V], F32, name="tb23", align_bytes=64)
         wraw = [sb.tile([P, PACK, HALF], F32, name="wraw%d" % h, align_bytes=64) for h in range(HALVES)]
         rst = sb.tile([P, PACK, J], F32, name="rst", align_bytes=64)
         gmt = sb.tile([P, PACK], F32, name="gmt", align_bytes=64)
         ident = sb.tile([P, P], F32, name="ident", align_bytes=64)
 
-        nc.vector.memset(xs[:].rearrange("p z c -> p (z c)").bitcast(I32), 0)
+        nc.gpsimd.memset(xs[:].rearrange("p z c -> p (z c)").bitcast(I32), 0)
         nc.vector.memset(ws[:].rearrange("p z c -> p (z c)").bitcast(I32), 0)
 
-        nc.sync.dma_start(idx[:], offs)
-        for z in range(PASSES):
-            nc.sync.dma_start(xw[z][:].bitcast(I32), xt_words[z].bitcast(I32))
-        for q in range(4):
-            nc.scalar.dma_start(
-                xs[32 * q : 32 * q + 4, :, :].bitcast(I32),
-                xt_scales[:, 4 * q : 4 * q + 4, :].rearrange("z r c -> r z c").bitcast(I32),
+        def load_scales(queue, plane, scales, q):
+            queue.dma_start(
+                plane[32 * q : 32 * q + 4, :, :].bitcast(I32),
+                scales[:, 4 * q : 4 * q + 4, :].rearrange("z r c -> r z c").bitcast(I32),
             )
+
+        tb_rows = tb.rearrange("(p t) v -> p t v", t=PACK)
+        wb_rows = wb.rearrange("(p i) n -> p i n", i=PACK)
+        nc.sync.dma_start(idx[:], offs)
+        nc.sync.dma_start(
+            xw[:].bitcast(I32).rearrange("p (z c) -> p z c", z=PASSES), xt_words.rearrange("z p c -> p z c").bitcast(I32)
+        )
+        for q in range(4):
+            load_scales(nc.sync, xs, xt_scales, q)
+        nc.sync.dma_start(wraw[0][:], wb_rows[:, :, 0:HALF])
         nc.sync.dma_start(ww[:].bitcast(I32), w_words.rearrange("z p c r -> p z (c r)").bitcast(I32))
         for q in range(4):
-            queue = nc.gpsimd if q < 2 else nc.scalar
-            queue.dma_start(
-                ws[32 * q : 32 * q + 4, :, :].bitcast(I32),
-                w_scales[:, 4 * q : 4 * q + 4, :].rearrange("z r c -> r z c").bitcast(I32),
-            )
-        tb_rows = tb.rearrange("(p t) v -> p t v", t=PACK)
-        nc.sync.dma_start(tbt[0][:], tb_rows[:, 0, :])
+            load_scales(nc.gpsimd if q == 0 else nc.sync, ws, w_scales, q)
         nc.sync.dma_start(idx3[:], offs3)
         nc.sync.dma_start(idx2[:], offs2)
-        for t in range(1, PACK):
-            nc.sync.dma_start(tbt[t][:], tb_rows[:, t, :])
-        wb_rows = wb.rearrange("(p i) n -> p i n", i=PACK)
-        for h in range(HALVES):
-            nc.sync.dma_start(wraw[h][:], wb_rows[:, :, h * HALF : (h + 1) * HALF])
+        nc.sync.dma_start(tb01[:], tb_rows[:, 0:2, :])
+        nc.sync.dma_start(tb23[:], tb_rows[:, 2:4, :])
+        nc.sync.dma_start(wraw[1][:], wb_rows[:, :, HALF:N])
         nc.sync.dma_start(rst[:], rs.rearrange("(p t) j -> p t j", t=PACK))
         nc.sync.dma_start(gmt[:], gm.rearrange("(p t) o -> p (t o)", t=PACK))
         make_identity(nc, ident[:])
 
         xg = sb.tile([P, PASSES, J], U16, name="xg", align_bytes=64)
         xsg = sb.tile([P, PASSES, J], U8, name="xsg", align_bytes=64)
-        for z in range(PASSES):
-            nc.vector.tensor_copy(xg[:, z, :], xw[z][:].indirect(idx[:]))
+        nc.vector.tensor_copy(xw1[:].bitcast(I32), xw[:, T : 2 * T].bitcast(I32))
+        nc.vector.tensor_copy(xg[:, 0, :], xw[:].indirect(idx[:]))
+        nc.vector.tensor_copy(xg[:, 1, :], xw1[:].indirect(idx[:]))
         for z in range(PASSES):
             nc.vector.tensor_copy(xsg[:, z, :], xs[:, z, :].indirect(idx[:]))
         a_jr = ps.tile([P, R], F32, name="a_jr")
@@ -95,42 +98,53 @@ def tile_list_picked_tworeach_residual_pl_kernel(
                 start=(z == 0),
                 stop=(z == PASSES - 1),
             )
-        g3 = sb.tile([P, PACK, J], F32, name="g3", align_bytes=64)
-        d = sb.tile([P, PACK, J], F32, name="d", align_bytes=64)
-        a_dealt = sb.tile([P, PACK, P], F32, name="a_dealt", align_bytes=64)
-        for t in range(PACK):
-            nc.scalar.activation(g3[:, t, :], tbt[t][:].indirect(idx3[:]), COPY)
-            nc.vector.tensor_tensor(d[:, t, :], tbt[t][:].indirect(idx2[:]), g3[:, t, :], ALU.subtract)
-        nc.scalar.copy(a_dealt[:], a_jr[:].rearrange("j (m t) -> j t m", t=PACK))
-        a_rj = ps.tile([P, PACK, J], F32, name="a_rj")
-        for t in range(PACK):
-            nc.tensor.transpose(a_rj[:, t, :], a_dealt[:, t, :], ident[:])
-        pre = sb.tile([P, PACK, J], F32, name="pre", align_bytes=64)
-        nc.vector.tensor_tensor(pre[:], a_rj[:], d[:], ALU.add)
-        hid = sb.tile([P, J, PACK], BF16, name="hid", align_bytes=64)
-        nc.vector.tensor_scalar_max(
-            hid[:].rearrange("p (c i) t -> p c t i", i=4), pre[:].rearrange("p t (c i) -> p c t i", i=4), 0.0
-        )
-        hq = sb.tile([P, J], U32, name="hq", align_bytes=64)
-        hs = sb.tile([P, J], U8, name="hs", align_bytes=64)
-        nc.vector.quantize_mx(out=hq[:].bitcast(E5M2), scales=hs[:], in_=hid[:].rearrange("p j t -> p (j t)"))
 
         wq = sb.tile([P, PACK, P], U32, name="wq", align_bytes=64)
         wqs = sb.tile([P, PACK, P], U8, name="wqs", align_bytes=64)
-        for h in range(HALVES):
-            wbf = sb.tile([P, PACK, HM, PACK], BF16, name="wbf%d" % h, align_bytes=64)
-            dst = wbf[:].rearrange("p t m i -> p m t i")
-            src = wraw[h][:].rearrange("p i (m t) -> p m t i", t=PACK)
-            if h == 0:
-                nc.scalar.copy(dst, src)
-            else:
-                nc.vector.tensor_copy(dst, src)
+        wbf = [sb.tile([P, PACK, HM, PACK], BF16, name="wbf%d" % h, align_bytes=64) for h in range(HALVES)]
+
+        def round_wb(copy, h, m0, m1):
+            copy(
+                wbf[h][:, :, m0:m1, :].rearrange("p t m i -> p m t i"),
+                wraw[h][:, :, PACK * m0 : PACK * m1].rearrange("p i (m t) -> p m t i", t=PACK),
+            )
+
+        def quantise_wb(h):
             for t in range(PACK):
                 nc.vector.quantize_mx(
                     out=wq[:, t, h * HM : (h + 1) * HM].bitcast(E4M3),
                     scales=wqs[:, t, h * HM : (h + 1) * HM],
-                    in_=wbf[:, t, :, :].rearrange("p m i -> p (m i)"),
+                    in_=wbf[h][:, t, :, :].rearrange("p m i -> p (m i)"),
                 )
+
+        round_wb(nc.scalar.copy, 0, 0, HM)
+        quantise_wb(0)
+
+        g3 = sb.tile([P, PACK, J], F32, name="g3", align_bytes=64)
+        g2 = sb.tile([P, PACK, J], F32, name="g2", align_bytes=64)
+        a_dealt = sb.tile([P, PACK, P], F32, name="a_dealt", align_bytes=64)
+        nc.scalar.copy(a_dealt[:], a_jr[:].rearrange("j (m t) -> j t m", t=PACK))
+        a_rj = ps.tile([P, PACK, J], F32, name="a_rj")
+        for t in range(PACK):
+            nc.tensor.transpose(a_rj[:, t, :], a_dealt[:, t, :], ident[:])
+        for t in range(PACK):
+            window = (tb01 if t < 2 else tb23)[:, t % 2, :]
+            nc.scalar.activation(g3[:, t, :], window.indirect(idx3[:]), COPY)
+            nc.vector.tensor_copy(g2[:, t, :], window.indirect(idx2[:]))
+        plus = sb.tile([P, PACK, J], F32, name="plus", align_bytes=64)
+        pre = sb.tile([P, PACK, J], F32, name="pre", align_bytes=64)
+        nc.vector.tensor_tensor(plus[:], a_rj[:], g2[:], ALU.add)
+        nc.vector.tensor_tensor(pre[:], plus[:], g3[:], ALU.subtract)
+        round_wb(nc.scalar.copy, 1, 0, HM // 2)
+        round_wb(nc.vector.tensor_copy, 1, HM // 2, HM)
+        hid = sb.tile([P, J, PACK], BF16, name="hid", align_bytes=64)
+        nc.scalar.activation(
+            hid[:].rearrange("p (c i) t -> p c t i", i=4), pre[:].rearrange("p t (c i) -> p c t i", i=4), RELU
+        )
+        quantise_wb(1)
+        hq = sb.tile([P, J], U32, name="hq", align_bytes=64)
+        hs = sb.tile([P, J], U8, name="hs", align_bytes=64)
+        nc.vector.quantize_mx(out=hq[:].bitcast(E5M2), scales=hs[:], in_=hid[:].rearrange("p j t -> p (j t)"))
 
         y = sb.tile([P, PACK, J], F32, name="y", align_bytes=64)
         for t in range(PACK):

from contextlib import ExitStack

import concourse.mybir as mybir
from concourse.masks import make_identity

K, T, J, R, V, N = 1024, 512, 128, 512, 512, 512
FLOPS = 2 * K * R * J + 2 * R * N * J

F32 = mybir.dt.float32
BF16 = mybir.dt.bfloat16
I32 = mybir.dt.int32
U32 = mybir.dt.uint32
U16 = mybir.dt.uint16
U8 = mybir.dt.uint8
E4M3 = mybir.dt.float8_e4m3fn_x4
E5M2 = mybir.dt.float8_e5m2_x4
E2M1 = mybir.dt.float4_e2m1fn_x4
ALU = mybir.AluOpType
COPY = mybir.ActivationFunctionType.Copy
RELU = mybir.ActivationFunctionType.Relu

P = 128
PACK = 4
PASSES = K // (P * PACK)
HALVES = 2
HALF = N // HALVES
HM = HALF // PACK


def tile_list_picked_tworeach_residual_pl_kernel(
    tc, xt_words, xt_scales, w_words, w_scales, tb, wb, rs, gm, offs, offs2, offs3, out_0, out_1, out_2
):
    nc = tc.nc
    with ExitStack() as ctx:
        sb = ctx.enter_context(tc.tile_pool(name="sb", bufs=1))
        ps = ctx.enter_context(tc.psum_pool(name="ps", bufs=1))

        idx = sb.tile([P, J // 16], U16, name="idx")
        idx2 = sb.tile([P, J // 16], U16, name="idx2")
        idx3 = sb.tile([P, J // 16], U16, name="idx3")
        xw = sb.tile([P, PASSES * T], U16, name="xw", align_bytes=64)
        xw1 = sb.tile([P, T], U16, name="xw1", align_bytes=64)
        xs = sb.tile([P, PASSES, T], U8, name="xs", align_bytes=64)
        ww = sb.tile([P, PASSES, R], U32, name="ww", align_bytes=64)
        ws = sb.tile([P, PASSES, R], U8, name="ws", align_bytes=64)
        tb01 = sb.tile([P, 2, V], F32, name="tb01", align_bytes=64)
        tb23 = sb.tile([P, 2, V], F32, name="tb23", align_bytes=64)
        wraw = [sb.tile([P, PACK, HALF], F32, name="wraw%d" % h, align_bytes=64) for h in range(HALVES)]
        rst = sb.tile([P, PACK, J], F32, name="rst", align_bytes=64)
        gmt = sb.tile([P, PACK], F32, name="gmt", align_bytes=64)
        ident = sb.tile([P, P], F32, name="ident", align_bytes=64)

        nc.gpsimd.memset(xs[:].rearrange("p z c -> p (z c)").bitcast(I32), 0)
        nc.vector.memset(ws[:].rearrange("p z c -> p (z c)").bitcast(I32), 0)

        def load_scales(queue, plane, scales, q):
            queue.dma_start(
                plane[32 * q : 32 * q + 4, :, :].bitcast(I32),
                scales[:, 4 * q : 4 * q + 4, :].rearrange("z r c -> r z c").bitcast(I32),
            )

        tb_rows = tb.rearrange("(p t) v -> p t v", t=PACK)
        wb_rows = wb.rearrange("(p i) n -> p i n", i=PACK)
        nc.sync.dma_start(idx[:], offs)
        nc.sync.dma_start(
            xw[:].bitcast(I32).rearrange("p (z c) -> p z c", z=PASSES), xt_words.rearrange("z p c -> p z c").bitcast(I32)
        )
        for q in range(4):
            load_scales(nc.sync, xs, xt_scales, q)
        nc.sync.dma_start(wraw[0][:], wb_rows[:, :, 0:HALF])
        nc.sync.dma_start(ww[:].bitcast(I32), w_words.rearrange("z p c r -> p z (c r)").bitcast(I32))
        for q in range(4):
            load_scales(nc.gpsimd if q == 0 else nc.sync, ws, w_scales, q)
        nc.sync.dma_start(idx3[:], offs3)
        nc.sync.dma_start(idx2[:], offs2)
        nc.sync.dma_start(tb01[:], tb_rows[:, 0:2, :])
        nc.sync.dma_start(tb23[:], tb_rows[:, 2:4, :])
        nc.sync.dma_start(wraw[1][:], wb_rows[:, :, HALF:N])
        nc.sync.dma_start(rst[:], rs.rearrange("(p t) j -> p t j", t=PACK))
        nc.sync.dma_start(gmt[:], gm.rearrange("(p t) o -> p (t o)", t=PACK))
        make_identity(nc, ident[:])

        xg = sb.tile([P, PASSES, J], U16, name="xg", align_bytes=64)
        xsg = sb.tile([P, PASSES, J], U8, name="xsg", align_bytes=64)
        nc.vector.tensor_copy(xw1[:].bitcast(I32), xw[:, T : 2 * T].bitcast(I32))
        nc.vector.tensor_copy(xg[:, 0, :], xw[:].indirect(idx[:]))
        nc.vector.tensor_copy(xg[:, 1, :], xw1[:].indirect(idx[:]))
        for z in range(PASSES):
            nc.vector.tensor_copy(xsg[:, z, :], xs[:, z, :].indirect(idx[:]))
        a_jr = ps.tile([P, R], F32, name="a_jr")
        for z in range(PASSES):
            nc.tensor.matmul_mx(
                out=a_jr[:],
                lhsT=xg[:, z, :].bitcast(E2M1),
                lhsT_scale=xsg[:, z, :],
                rhs=ww[:, z, :].bitcast(E5M2),
                rhs_scale=ws[:, z, :],
                start=(z == 0),
                stop=(z == PASSES - 1),
            )

        wq = sb.tile([P, PACK, P], U32, name="wq", align_bytes=64)
        wqs = sb.tile([P, PACK, P], U8, name="wqs", align_bytes=64)
        wbf = [sb.tile([P, PACK, HM, PACK], BF16, name="wbf%d" % h, align_bytes=64) for h in range(HALVES)]

        def round_wb(copy, h, m0, m1):
            copy(
                wbf[h][:, :, m0:m1, :].rearrange("p t m i -> p m t i"),
                wraw[h][:, :, PACK * m0 : PACK * m1].rearrange("p i (m t) -> p m t i", t=PACK),
            )

        def quantise_wb(h):
            for t in range(PACK):
                nc.vector.quantize_mx(
                    out=wq[:, t, h * HM : (h + 1) * HM].bitcast(E4M3),
                    scales=wqs[:, t, h * HM : (h + 1) * HM],
                    in_=wbf[h][:, t, :, :].rearrange("p m i -> p (m i)"),
                )

        round_wb(nc.scalar.copy, 0, 0, HM)
        quantise_wb(0)

        g3 = sb.tile([P, PACK, J], F32, name="g3", align_bytes=64)
        g2 = sb.tile([P, PACK, J], F32, name="g2", align_bytes=64)
        a_dealt = sb.tile([P, PACK, P], F32, name="a_dealt", align_bytes=64)
        nc.scalar.copy(a_dealt[:], a_jr[:].rearrange("j (m t) -> j t m", t=PACK))
        a_rj = ps.tile([P, PACK, J], F32, name="a_rj")
        for t in range(PACK):
            nc.tensor.transpose(a_rj[:, t, :], a_dealt[:, t, :], ident[:])
        for t in range(PACK):
            window = (tb01 if t < 2 else tb23)[:, t % 2, :]
            nc.scalar.activation(g3[:, t, :], window.indirect(idx3[:]), COPY)
            nc.vector.tensor_copy(g2[:, t, :], window.indirect(idx2[:]))
        plus = sb.tile([P, PACK, J], F32, name="plus", align_bytes=64)
        pre = sb.tile([P, PACK, J], F32, name="pre", align_bytes=64)
        nc.vector.tensor_tensor(plus[:], a_rj[:], g2[:], ALU.add)
        nc.vector.tensor_tensor(pre[:], plus[:], g3[:], ALU.subtract)
        round_wb(nc.scalar.copy, 1, 0, HM // 2)
        round_wb(nc.vector.tensor_copy, 1, HM // 2, HM)
        hid = sb.tile([P, J, PACK], BF16, name="hid", align_bytes=64)
        nc.scalar.activation(
            hid[:].rearrange("p (c i) t -> p c t i", i=4), pre[:].rearrange("p t (c i) -> p c t i", i=4), RELU
        )
        quantise_wb(1)
        hq = sb.tile([P, J], U32, name="hq", align_bytes=64)
        hs = sb.tile([P, J], U8, name="hs", align_bytes=64)
        nc.vector.quantize_mx(out=hq[:].bitcast(E5M2), scales=hs[:], in_=hid[:].rearrange("p j t -> p (j t)"))

        y = sb.tile([P, PACK, J], F32, name="y", align_bytes=64)
        for t in range(PACK):
            pt = ps.tile([P, J], F32, name="pt%d" % t)
            nc.tensor.matmul_mx(
                out=pt[:],
                lhsT=wq[:, t, :].bitcast(E4M3),
                lhsT_scale=wqs[:, t, :],
                rhs=hq[:].bitcast(E5M2),
                rhs_scale=hs[:],
                start=True,
                stop=True,
            )
            nc.vector.scalar_tensor_tensor(y[:, t, :], pt[:], gmt[:, t : t + 1], rst[:, t, :], ALU.mult, ALU.add)
        nc.sync.dma_start(out_0.rearrange("(p t) j -> p t j", t=PACK), y[:])
        yb = sb.tile([P, J, PACK], BF16, name="yb", align_bytes=64)
        nc.vector.tensor_copy(
            yb[:].rearrange("p (c i) t -> p c t i", i=4), y[:].rearrange("p t (c i) -> p c t i", i=4)
        )
        yq = sb.tile([P, J], U32, name="yq", align_bytes=64)
        ys = sb.tile([P, J], U8, name="ys", align_bytes=64)
        nc.vector.quantize_mx(out=yq[:].bitcast(E4M3), scales=ys[:], in_=yb[:].rearrange("p j t -> p (j t)"))
        nc.sync.dma_start(out_1[0].rearrange("p c r -> p (c r)").bitcast(I32), yq[:].bitcast(I32))
        for q in range(4):
            queue = nc.scalar if q % 2 == 0 else nc.sync
            queue.dma_start(out_2[0, 4 * q : 4 * q + 4, :].bitcast(I32), ys[32 * q : 32 * q + 4, :].bitcast(I32))
